import numpy as np
import ml_dtypes


def mxq(x, axis, fmt="e4m3"):
    dtype, down = {"e4m3": (ml_dtypes.float8_e4m3fn, 7), "e5m2": (ml_dtypes.float8_e5m2, 14)}[fmt]
    v = np.moveaxis(np.asarray(x, np.float32).astype(ml_dtypes.bfloat16).astype(np.float64), axis, -1)
    blocks = v.reshape(v.shape[:-1] + (-1, 32))
    amax = np.abs(blocks).max(-1, keepdims=True)
    byte = np.maximum(np.where(amax > 0, np.frexp(amax)[1] - 1 + 127, 0) - down, 1)
    scale = np.exp2(byte - 127.0)
    codes = (blocks / scale).astype(np.float32).astype(dtype).astype(np.float64)
    return np.moveaxis((codes * scale).reshape(v.shape), -1, axis)


WIDE = False


def mx_kscale(k):
    if not WIDE:
        return np.ones(k)
    levels = np.array([10, -10, 5, -5, 0])
    if k % 512:
        return np.exp2(np.random.permutation(np.resize(levels, k // 32))).repeat(32)
    a = np.empty((k // 512, 16))
    for p in range(k // 512):
        a[p, :8] = np.random.permutation(np.resize(levels, 8))
        for g in range(8):
            far = levels[np.abs(levels - a[p, g]) >= 10]
            a[p, g + 8] = far[np.random.randint(len(far))]
    return np.exp2(a.ravel()).repeat(32)


def f64(x):
    return np.asarray(x).astype(np.float64)


def striped(idx):
    return np.tile(idx.reshape(-1, 16).T, (8, 1)).astype(np.uint16)


def unstriped(offs):
    return offs[:16].T.reshape(-1).astype(np.int64)


def pack_weight(w):
    k, n = w.shape
    w = f64(np.asarray(w, np.float32).astype(ml_dtypes.bfloat16)).reshape(k // 32, 32, n)
    amax = np.abs(w).max(1)
    byte = np.clip(np.where(amax > 0, np.frexp(amax)[1] - 1 + 127 - 7, 1), 1, 254)
    scaled = (w * np.exp2(127.0 - byte)[:, None, :]).reshape(k, n).astype(np.float32)
    words = np.ascontiguousarray(scaled.reshape(k // 512, 128, 4, n).transpose(0, 1, 3, 2)).astype(ml_dtypes.float8_e4m3fn).view(np.uint8)
    return words, np.ascontiguousarray(byte.astype(np.uint8).reshape(k // 512, 16, n))


def unpack_weight(words, scales):
    g, p, n, _ = words.shape
    vals = np.ascontiguousarray(words).view(ml_dtypes.float8_e4m3fn).astype(np.float64) * np.repeat(np.exp2(scales.astype(np.float64) - 127.0), 8, axis=1)[..., None]
    return vals.transpose(0, 1, 3, 2).reshape(g * 512, n)


def planes(y):
    n, m = y.shape
    v = y.astype(np.float32).astype(ml_dtypes.bfloat16).astype(np.float64).reshape(n // 32, 32, m)
    top = np.abs(v).max(1)
    byte = np.clip(np.where(top > 0, np.frexp(top)[1] - 1 + 127 - 7, 1), 1, 254)
    codes = (v * np.exp2(127.0 - byte)[:, None, :]).reshape(n, m).astype(np.float32).astype(ml_dtypes.float8_e4m3fn).view(np.uint8)
    words = codes.reshape(n // 512, 128, 4, m).transpose(0, 1, 3, 2)
    return np.ascontiguousarray(words), np.ascontiguousarray(byte.astype(np.uint8).reshape(n // 512, 16, m))


K, T, S, N, H, W, G, U = 512, 2048, 512, 512, 512, 1024, 2048, 1024


def setup_inputs():
    n = np.random.standard_normal
    s = mx_kscale(K)[:, None]
    u = mx_kscale(H)
    packed_xT = pack_weight(n((K, T)) * s)
    packed_eT = pack_weight(n((K, W)) * s)
    packed_dT = pack_weight(n((K, G)) * s)
    return {
        "x_words": packed_xT[0],
        "x_scales": packed_xT[1],
        "w1": (n((K, N)) / np.sqrt(K) / s).astype(np.float32),
        "e_words": packed_eT[0],
        "e_scales": packed_eT[1],
        "w2": (n((K, N)) / np.sqrt(K) / s).astype(np.float32),
        "d_words": packed_dT[0],
        "d_scales": packed_dT[1],
        "w3": (n((K, N)) / np.sqrt(K) / s).astype(np.float32),
        "unit": (np.random.uniform(0.6, 1.4, (H, 1)) * u[:, None]).astype(np.float32),
        "w4": (n((H, N)) / np.sqrt(H) / u[:, None]).astype(np.float32),
        "offs": striped(np.random.permutation(T)[:S]),
        "prd": striped(np.random.permutation(W)[:S]),
        "obj": striped(np.random.permutation(G)[:S]),
        "ts": striped(np.random.permutation(np.concatenate([np.arange(S), np.random.randint(0, S, U - S)]))),
        "tp": striped(np.random.permutation(np.concatenate([np.arange(S), np.random.randint(0, S, U - S)]))),
        "to": striped(np.random.permutation(np.concatenate([np.arange(S), np.random.randint(0, S, U - S)]))),
    }


def reference(x_words, x_scales, w1, e_words, e_scales, w2, d_words, d_scales, w3, unit, w4, offs, prd, obj, ts, tp, to):
    xq = unpack_weight(x_words, x_scales)[:, unstriped(offs)]
    y = mxq(f64(w1), 0, "e4m3").T @ xq
    sb = y[:, unstriped(ts)]
    e_prd = unpack_weight(e_words, e_scales)[:, unstriped(prd)]
    ye = mxq(f64(w2), 0, "e4m3").T @ e_prd
    pr = ye[:, unstriped(tp)]
    hop = np.maximum(sb * pr, 0.4 * sb)
    d_obj = unpack_weight(d_words, d_scales)[:, unstriped(obj)]
    yd = mxq(f64(w3), 0, "e4m3").T @ d_obj
    ob = yd[:, unstriped(to)]
    hid = f64(unit) * (hop * ob)
    out_0 = mxq(f64(w4), 0, "e4m3").T @ mxq(hid, 0, "e4m3")
    return (out_0,) + planes(out_0)

@@ -1,0 +1,198 @@
+from contextlib import ExitStack
+
+import concourse.mybir as mybir
+
+K, S, U = 512, 512, 1024
+FLOPS = 2 * K * 512 * (3 * S + U)
+
+F32 = mybir.dt.float32
+BF16 = mybir.dt.bfloat16
+I32 = mybir.dt.int32
+U32 = mybir.dt.uint32
+U16 = mybir.dt.uint16
+U8 = mybir.dt.uint8
+FP8X4 = mybir.dt.float8_e4m3fn_x4
+COPY = mybir.ActivationFunctionType.Copy
+MULT = mybir.AluOpType.mult
+MAX = mybir.AluOpType.max
+
+P = 128
+PACK = 4
+CHUNK = 256
+LINE = 4
+
+
+def tile_picked_ytriple_mul_po_kernel(
+    tc, x_words, x_scales, w1, e_words, e_scales, w2, d_words, d_scales, w3, unit, w4,
+    offs, prd, obj, ts, tp, to, out_0, out_1, out_2,
+):
+    nc = tc.nc
+    with ExitStack() as ctx:
+        keep = ctx.enter_context(tc.tile_pool(name="keep", bufs=1))
+        psum = ctx.enter_context(tc.psum_pool(name="psum", bufs=4))
+
+        def load_list(name, src):
+            t = keep.tile(list(src.shape), U16, name=name)
+            nc.sync.dma_start(t[:], src)
+            return t
+
+        def load_weight(name, w):
+            raw = keep.tile([P, PACK, 512], F32, name=name + "_raw")
+            nc.sync.dma_start(raw[:], w.rearrange("(p j) c -> p j c", j=PACK))
+            return raw
+
+        def load_scales(name, scales, queue):
+            width = scales.shape[2]
+            plane = keep.tile([P, width], U8, name=name + "_plane", tag=name + "_plane", align_bytes=64)
+            nc.vector.memset(plane[:].bitcast(I32), 0)
+            for q in range(4):
+                queue.dma_start(plane[32 * q : 32 * q + 4, :].bitcast(I32), scales[0, 4 * q : 4 * q + 4, :].bitcast(I32))
+            return plane
+
+        def load_words(name, words):
+            width = words.shape[2]
+            table = keep.tile([P, width], I32, name=name + "_table", tag=name + "_table", align_bytes=64)
+            nc.sync.dma_start(table[:], words[0].rearrange("p n t -> p (n t)").bitcast(I32))
+            return table
+
+        w1_raw = load_weight("w1", w1)
+        offs_sb = load_list("offs", offs)
+        x_plane = load_scales("x", x_scales, nc.sync)
+        x_table = load_words("x", x_words)
+        e_table = load_words("e", e_words)
+        e_plane = load_scales("e", e_scales, nc.gpsimd)
+        d_plane = load_scales("d", d_scales, nc.gpsimd)
+        ts_sb = load_list("ts", ts)
+        prd_sb = load_list("prd", prd)
+        w2_raw = load_weight("w2", w2)
+        tp_sb = load_list("tp", tp)
+        obj_sb = load_list("obj", obj)
+        w3_raw = load_weight("w3", w3)
+        d_table = load_words("d", d_words)
+        unit_sb = keep.tile([P, PACK], F32, name="unit_sb")
+        nc.sync.dma_start(unit_sb[:], unit.rearrange("(p t) o -> p (t o)", t=PACK))
+        to_sb = load_list("to", to)
+        w4_raw = load_weight("w4", w4)
+
+        def round_weight(name, raw, vector_cols, tag):
+            grouped = keep.tile([P, PACK, P, PACK], BF16, name=name + "_bf16", tag=tag, align_bytes=64)
+            dst = grouped[:].rearrange("p t m j -> p m j t")
+            src = raw[:].rearrange("p j (m t) -> p m j t", t=PACK)
+            if vector_cols < P:
+                nc.scalar.copy(dst[:, vector_cols:], src[:, vector_cols:])
+            if vector_cols > 0:
+                nc.vector.tensor_copy(dst[:, :vector_cols], src[:, :vector_cols])
+            return grouped
+
+        def quantize_weight(name, grouped):
+            codes = keep.tile([P, 512], U32, name=name + "_codes", align_bytes=64)
+            scales = keep.tile([P, 512], U8, name=name + "_scales", align_bytes=64)
+            nc.vector.quantize_mx(codes[:].bitcast(FP8X4), scales[:], grouped[:].rearrange("p t m j -> p (t m j)"))
+            return codes, scales
+
+        def pick(name, table, plane, lst):
+            scales = keep.tile([P, S], U8, name=name + "_picked_scales", align_bytes=64)
+            nc.vector.tensor_copy(scales[:], plane[:].indirect(lst[:]))
+            words = keep.tile([P, S], U32, name=name + "_picked_words", tag=name + "_picked", align_bytes=64)
+            nc.vector.tensor_copy(words[:], table[:].bitcast(U32).indirect(lst[:]))
+            return words, scales
+
+        def product(name, wq, picked, row_scale):
+            rows = []
+            for t in range(PACK):
+                cols = slice(P * t, P * (t + 1))
+                bank = psum.tile([P, S], F32, name="first_bank")
+                nc.tensor.matmul_mx(
+                    bank[:], lhsT=wq[0][:, cols].bitcast(FP8X4), lhsT_scale=wq[1][:, cols],
+                    rhs=picked[0][:].bitcast(FP8X4), rhs_scale=picked[1][:], start=True, stop=True,
+                )
+                row = keep.tile([P, S], F32, name=f"{name}_{t}")
+                if row_scale is None:
+                    nc.scalar.copy(row[:], bank[:])
+                else:
+                    nc.scalar.activation(row[:], bank[:], COPY, scale=row_scale[:, t : t + 1])
+                rows.append(row)
+            return rows
+
+        w1q = quantize_weight("w1", round_weight("w1", w1_raw, 64, "w1_bf16"))
+        y = product("y", w1q, pick("x", x_table, x_plane, offs_sb), None)
+        e_picked = pick("e", e_table, e_plane, prd_sb)
+        w2q = quantize_weight("w2", round_weight("w2", w2_raw, 128, "w2_bf16"))
+        ye = product("ye", w2q, e_picked, None)
+        w3q = quantize_weight("w3", round_weight("w3", w3_raw, 128, "w3_bf16"))
+        yd = product("yd", w3q, pick("d", d_table, d_plane, obj_sb), unit_sb)
+
+        out_scales = keep.tile([P, U], U8, name="out_scales", align_bytes=64)
+        out_rows = out_0.rearrange("(p t) r -> p t r", t=PACK)
+        out_words = out_1[0].rearrange("p n t -> p (n t)").bitcast(I32)
+
+        def by_lines(planes):
+            return planes.rearrange("p t (c i) -> p c t i", i=LINE)
+
+        def grouped_by_lines(grouped):
+            return grouped.rearrange("p (c i) t -> p c t i", i=LINE)
+
+        chunks = range(U // CHUNK)
+        entries = [slice(c * CHUNK // 16, (c + 1) * CHUNK // 16) for c in chunks]
+        facts = [slice(c * CHUNK, (c + 1) * CHUNK) for c in chunks]
+        sb_first = keep.tile([P, PACK, CHUNK], F32, name="sb_first")
+        sb_second = keep.tile([P, PACK, CHUNK], F32, name="sb_second", tag="e_picked", align_bytes=64)
+        sb_rest = keep.tile([P, 2, PACK, CHUNK], F32, name="sb_rest", tag="d_picked", align_bytes=64)
+        sb = [sb_first[:], sb_second[:], sb_rest[:, 0], sb_rest[:, 1]]
+        hop_all = keep.tile([P, U // CHUNK, PACK, CHUNK], F32, name="hop_all", tag="d_table", align_bytes=64)
+        hop = [hop_all[:, c] for c in chunks]
+        ob = [keep.tile([P, PACK, CHUNK], F32, name=f"ob_{c}") for c in chunks]
+        for c in chunks:
+            for t in range(PACK):
+                nc.scalar.activation(sb[c][:, t, :], y[t][:].indirect(ts_sb[:, entries[c]]), COPY)
+            for t in range(PACK):
+                nc.vector.tensor_tensor(hop[c][:, t, :], ye[t][:].indirect(tp_sb[:, entries[c]]), sb[c][:, t, :], MULT)
+            if c > 0:
+                nc.vector.scalar_tensor_tensor(hop[c - 1], sb[c - 1], 0.4, hop[c - 1], MULT, MAX)
+        nc.vector.scalar_tensor_tensor(hop[-1], sb[-1], 0.4, hop[-1], MULT, MAX)
+        w4q = quantize_weight("w4", round_weight("w4", w4_raw, 64, "d_plane"))
+        for c in chunks:
+            for t in range(PACK):
+                nc.scalar.activation(ob[c][:, t, :], yd[t][:].indirect(to_sb[:, entries[c]]), COPY)
+        hid = [keep.tile([P, CHUNK, PACK], BF16, name=f"hid_{c}", align_bytes=64) for c in chunks]
+        hid_codes = [keep.tile([P, CHUNK], U32, name=f"hid_codes_{c}", align_bytes=64) for c in chunks]
+        hid_scales = [keep.tile([P, CHUNK], U8, name=f"hid_scales_{c}", align_bytes=64) for c in chunks]
+        res = [keep.tile([P, PACK, CHUNK], F32, name=f"res_{c}") for c in chunks]
+        res_bf = [keep.tile([P, CHUNK, PACK], BF16, name=f"res_bf_{c}", align_bytes=64) for c in chunks]
+        res_codes = [keep.tile([P, CHUNK], I32, name=f"res_codes_{c}", align_bytes=64) for c in chunks]
+
+        def make_hid(c):
+            nc.vector.tensor_tensor(grouped_by_lines(hid[c][:]), by_lines(hop[c]), by_lines(ob[c][:]), MULT)
+
+        def last_product(c):
+            nc.vector.quantize_mx(hid_codes[c][:].bitcast(FP8X4), hid_scales[c][:], hid[c][:].rearrange("p c t -> p (c t)"))
+            for half in range(2):
+                bank = psum.tile([P, 2, CHUNK], F32, name="last_bank")
+                for k in range(2):
+                    cols = slice(P * (2 * half + k), P * (2 * half + k + 1))
+                    nc.tensor.matmul_mx(
+                        bank[:, k, :], lhsT=w4q[0][:, cols].bitcast(FP8X4), lhsT_scale=w4q[1][:, cols],
+                        rhs=hid_codes[c][:].bitcast(FP8X4), rhs_scale=hid_scales[c][:], start=True, stop=True,
+                    )
+                nc.scalar.copy(res[c][:, 2 * half : 2 * half + 2, :], bank[:])
+            nc.sync.dma_start(out_rows[:, :, facts[c]], res[c][:])
+
+        def round_res(c):
+            nc.vector.tensor_copy(grouped_by_lines(res_bf[c][:]), by_lines(res[c][:]))
+
+        def quantize_res(c):
+            nc.vector.quantize_mx(res_codes[c][:].bitcast(FP8X4), out_scales[:, facts[c]], res_bf[c][:].rearrange("p c t -> p (c t)"))
+            nc.sync.dma_start(out_words[:, facts[c]], res_codes[c][:])
+
+        make_hid(0)
+        for c in chunks:
+            if c + 1 < len(chunks):
+                make_hid(c + 1)
+            last_product(c)
+        round_res(0)
+        for c in chunks:
+            if c + 1 < len(chunks):
+                round_res(c + 1)
+            quantize_res(c)
+        for q in range(4):
+            nc.sync.dma_start(out_2[0, 4 * q : 4 * q + 4, :].bitcast(I32), out_scales[32 * q : 32 * q + 4, :].bitcast(I32))

@@ -18,8 +18,10 @@ MAX = mybir.AluOpType.max
 
 P = 128
 PACK = 4
-CHUNK = 256
-LINE = 4
+CHUNKS = (slice(0, 512), slice(512, 768), slice(768, 1024))
+HALF = 512
+PAIR = 2
+SPARE = 16
 
 
 def tile_picked_ytriple_mul_po_kernel(
@@ -29,7 +31,7 @@ def tile_picked_ytriple_mul_po_kernel(
     nc = tc.nc
     with ExitStack() as ctx:
         keep = ctx.enter_context(tc.tile_pool(name="keep", bufs=1))
-        psum = ctx.enter_context(tc.psum_pool(name="psum", bufs=4))
+        psum = ctx.enter_context(tc.psum_pool(name="psum", bufs=8))
 
         def load_list(name, src):
             t = keep.tile(list(src.shape), U16, name=name)
@@ -37,14 +39,15 @@ def tile_picked_ytriple_mul_po_kernel(
             return t
 
         def load_weight(name, w):
-            raw = keep.tile([P, PACK, 512], F32, name=name + "_raw")
+            raw = keep.tile([P, PACK, w.shape[1]], F32, name=name + "_raw", tag=name + "_raw")
             nc.sync.dma_start(raw[:], w.rearrange("(p j) c -> p j c", j=PACK))
             return raw
 
         def load_scales(name, scales, queue):
             width = scales.shape[2]
             plane = keep.tile([P, width], U8, name=name + "_plane", tag=name + "_plane", align_bytes=64)
-            nc.vector.memset(plane[:].bitcast(I32), 0)
+            nc.vector.memset(plane[:, : width // 2].bitcast(I32), 0)
+            nc.gpsimd.memset(plane[:, width // 2 :].bitcast(I32), 0)
             for q in range(4):
                 queue.dma_start(plane[32 * q : 32 * q + 4, :].bitcast(I32), scales[0, 4 * q : 4 * q + 4, :].bitcast(I32))
             return plane
@@ -55,33 +58,34 @@ def tile_picked_ytriple_mul_po_kernel(
             nc.sync.dma_start(table[:], words[0].rearrange("p n t -> p (n t)").bitcast(I32))
             return table
 
-        w1_raw = load_weight("w1", w1)
+        w1_low = load_weight("w1_low", w1[:, :256])
+        w1_high = load_weight("w1_high", w1[:, 256:])
         offs_sb = load_list("offs", offs)
         x_plane = load_scales("x", x_scales, nc.sync)
         x_table = load_words("x", x_words)
         e_table = load_words("e", e_words)
-        e_plane = load_scales("e", e_scales, nc.gpsimd)
-        d_plane = load_scales("d", d_scales, nc.gpsimd)
-        ts_sb = load_list("ts", ts)
         prd_sb = load_list("prd", prd)
+        e_plane = load_scales("e", e_scales, nc.sync)
         w2_raw = load_weight("w2", w2)
+        ts_sb = load_list("ts", ts)
         tp_sb = load_list("tp", tp)
-        obj_sb = load_list("obj", obj)
         w3_raw = load_weight("w3", w3)
+        obj_sb = load_list("obj", obj)
+        d_plane = load_scales("d", d_scales, nc.sync)
         d_table = load_words("d", d_words)
         unit_sb = keep.tile([P, PACK], F32, name="unit_sb")
         nc.sync.dma_start(unit_sb[:], unit.rearrange("(p t) o -> p (t o)", t=PACK))
         to_sb = load_list("to", to)
         w4_raw = load_weight("w4", w4)
 
-        def round_weight(name, raw, vector_cols, tag):
+        def round_weight(name, pieces, tag):
             grouped = keep.tile([P, PACK, P, PACK], BF16, name=name + "_bf16", tag=tag, align_bytes=64)
             dst = grouped[:].rearrange("p t m j -> p m j t")
-            src = raw[:].rearrange("p j (m t) -> p m j t", t=PACK)
-            if vector_cols < P:
-                nc.scalar.copy(dst[:, vector_cols:], src[:, vector_cols:])
-            if vector_cols > 0:
-                nc.vector.tensor_copy(dst[:, :vector_cols], src[:, :vector_cols])
+            first = 0
+            for raw, copy in pieces:
+                src = raw[:].rearrange("p j (m t) -> p m j t", t=PACK)
+                copy(dst[:, first : first + src.shape[1]], src)
+                first = first + src.shape[1]
             return grouped
 
         def quantize_weight(name, grouped):
@@ -97,102 +101,114 @@ def tile_picked_ytriple_mul_po_kernel(
             nc.vector.tensor_copy(words[:], table[:].bitcast(U32).indirect(lst[:]))
             return words, scales
 
-        def product(name, wq, picked, row_scale):
+        def product(name, wq, picked, row_scale, offsets_at_once):
             rows = []
             for t in range(PACK):
                 cols = slice(P * t, P * (t + 1))
-                bank = psum.tile([P, S], F32, name="first_bank")
+                bank = psum.tile([P, S], F32, name="bank")
                 nc.tensor.matmul_mx(
                     bank[:], lhsT=wq[0][:, cols].bitcast(FP8X4), lhsT_scale=wq[1][:, cols],
                     rhs=picked[0][:].bitcast(FP8X4), rhs_scale=picked[1][:], start=True, stop=True,
                 )
-                row = keep.tile([P, S], F32, name=f"{name}_{t}")
+                row = keep.tile([P, offsets_at_once + SPARE], F32, name=f"{name}_{t}")
+                nc.gpsimd.memset(row[:, S:], 0.0)
                 if row_scale is None:
-                    nc.scalar.copy(row[:], bank[:])
+                    nc.scalar.copy(row[:, :S], bank[:])
                 else:
-                    nc.scalar.activation(row[:], bank[:], COPY, scale=row_scale[:, t : t + 1])
+                    nc.scalar.activation(row[:, :S], bank[:], COPY, scale=row_scale[:, t : t + 1])
                 rows.append(row)
             return rows
 
-        w1q = quantize_weight("w1", round_weight("w1", w1_raw, 64, "w1_bf16"))
-        y = product("y", w1q, pick("x", x_table, x_plane, offs_sb), None)
+        w1q = quantize_weight("w1", round_weight("w1", [(w1_low, nc.scalar.copy), (w1_high, nc.vector.tensor_copy)], "w1_bf16"))
+        y = product("y", w1q, pick("x", x_table, x_plane, offs_sb), None, U)
         e_picked = pick("e", e_table, e_plane, prd_sb)
-        w2q = quantize_weight("w2", round_weight("w2", w2_raw, 128, "w2_bf16"))
-        ye = product("ye", w2q, e_picked, None)
-        w3q = quantize_weight("w3", round_weight("w3", w3_raw, 128, "w3_bf16"))
-        yd = product("yd", w3q, pick("d", d_table, d_plane, obj_sb), unit_sb)
+        w2q = quantize_weight("w2", round_weight("w2", [(w2_raw, nc.vector.tensor_copy)], "w2_bf16"))
+        ye = product("ye", w2q, e_picked, None, U)
+        w3q = quantize_weight("w3", round_weight("w3", [(w3_raw, nc.vector.tensor_copy)], "w3_bf16"))
+
+        sb_first = keep.tile([P, U], F32, name="sb_first")
+        sb_rest = keep.tile([P, PACK - 1, U], F32, name="sb_rest", tag="e_picked", align_bytes=64)
+        sb = [sb_first[:]] + [sb_rest[:, t, :] for t in range(PACK - 1)]
+        early = keep.tile([P, U], F32, name="early", tag="w3_bf16", align_bytes=64)
+        hop = keep.tile([P, PACK, U], F32, name="hop")
+        ob = [keep.tile([P, PACK, HALF], F32, name=f"ob_{h}") for h in range(U // HALF)]
+        for t in range(PACK):
+            nc.scalar.activation(sb[t], y[t][:].indirect(ts_sb[:]), COPY)
+
+        def times_predicate(t, dst):
+            nc.vector.tensor_tensor(dst, ye[t][:].indirect(tp_sb[:]), sb[t], MULT)
+
+        def larger(t, prod):
+            nc.vector.scalar_tensor_tensor(hop[:, t, :], sb[t], 0.4, prod, MULT, MAX)
+
+        times_predicate(0, early[:])
+        d_picked = pick("d", d_table, d_plane, obj_sb)
+        w4_bf16 = round_weight("w4", [(w4_raw, nc.scalar.copy)], "d_plane")
+        yd = product("yd", w3q, d_picked, unit_sb, HALF)
+        late = keep.tile([P, PACK - 1, U], F32, name="late", tag="d_table", align_bytes=64)
+        products = [early[:]] + [late[:, t, :] for t in range(PACK - 1)]
+        for t in range(1, PACK):
+            times_predicate(t, products[t])
+            larger(t - 1, products[t - 1])
+        w4q = quantize_weight("w4", w4_bf16)
+        larger(PACK - 1, products[PACK - 1])
+        for first in range(0, U, HALF):
+            for t in range(PACK):
+                nc.scalar.activation(ob[first // HALF][:, t, :], yd[t][:].indirect(to_sb[:, first // 16 : (first + HALF) // 16]), COPY)
 
         out_scales = keep.tile([P, U], U8, name="out_scales", align_bytes=64)
         out_rows = out_0.rearrange("(p t) r -> p t r", t=PACK)
         out_words = out_1[0].rearrange("p n t -> p (n t)").bitcast(I32)
 
-        def by_lines(planes):
-            return planes.rearrange("p t (c i) -> p c t i", i=LINE)
+        def by_pairs(planes):
+            return planes.rearrange("p t (c i) -> p c t i", i=PAIR)
 
-        def grouped_by_lines(grouped):
-            return grouped.rearrange("p (c i) t -> p c t i", i=LINE)
+        def grouped_by_pairs(grouped):
+            return grouped.rearrange("p (c i) t -> p c t i", i=PAIR)
 
-        chunks = range(U // CHUNK)
-        entries = [slice(c * CHUNK // 16, (c + 1) * CHUNK // 16) for c in chunks]
-        facts = [slice(c * CHUNK, (c + 1) * CHUNK) for c in chunks]
-        sb_first = keep.tile([P, PACK, CHUNK], F32, name="sb_first")
-        sb_second = keep.tile([P, PACK, CHUNK], F32, name="sb_second", tag="e_picked", align_bytes=64)
-        sb_rest = keep.tile([P, 2, PACK, CHUNK], F32, name="sb_rest", tag="d_picked", align_bytes=64)
-        sb = [sb_first[:], sb_second[:], sb_rest[:, 0], sb_rest[:, 1]]
-        hop_all = keep.tile([P, U // CHUNK, PACK, CHUNK], F32, name="hop_all", tag="d_table", align_bytes=64)
-        hop = [hop_all[:, c] for c in chunks]
-        ob = [keep.tile([P, PACK, CHUNK], F32, name=f"ob_{c}") for c in chunks]
-        for c in chunks:
-            for t in range(PACK):
-                nc.scalar.activation(sb[c][:, t, :], y[t][:].indirect(ts_sb[:, entries[c]]), COPY)
-            for t in range(PACK):
-                nc.vector.tensor_tensor(hop[c][:, t, :], ye[t][:].indirect(tp_sb[:, entries[c]]), sb[c][:, t, :], MULT)
-            if c > 0:
-                nc.vector.scalar_tensor_tensor(hop[c - 1], sb[c - 1], 0.4, hop[c - 1], MULT, MAX)
-        nc.vector.scalar_tensor_tensor(hop[-1], sb[-1], 0.4, hop[-1], MULT, MAX)
-        w4q = quantize_weight("w4", round_weight("w4", w4_raw, 64, "d_plane"))
-        for c in chunks:
-            for t in range(PACK):
-                nc.scalar.activation(ob[c][:, t, :], yd[t][:].indirect(to_sb[:, entries[c]]), COPY)
-        hid = [keep.tile([P, CHUNK, PACK], BF16, name=f"hid_{c}", align_bytes=64) for c in chunks]
-        hid_codes = [keep.tile([P, CHUNK], U32, name=f"hid_codes_{c}", align_bytes=64) for c in chunks]
-        hid_scales = [keep.tile([P, CHUNK], U8, name=f"hid_scales_{c}", align_bytes=64) for c in chunks]
-        res = [keep.tile([P, PACK, CHUNK], F32, name=f"res_{c}") for c in chunks]
-        res_bf = [keep.tile([P, CHUNK, PACK], BF16, name=f"res_bf_{c}", align_bytes=64) for c in chunks]
-        res_codes = [keep.tile([P, CHUNK], I32, name=f"res_codes_{c}", align_bytes=64) for c in chunks]
+        widths = [facts.stop - facts.start for facts in CHUNKS]
+        hid = [keep.tile([P, w, PACK], BF16, name=f"hid_{c}", align_bytes=64) for c, w in enumerate(widths)]
+        hid_codes = [keep.tile([P, w], U32, name=f"hid_codes_{c}", align_bytes=64) for c, w in enumerate(widths)]
+        hid_scales = [keep.tile([P, w], U8, name=f"hid_scales_{c}", align_bytes=64) for c, w in enumerate(widths)]
+        res = [keep.tile([P, PACK, w], F32, name=f"res_{c}", tag=("w2_raw", "w1_low_raw", "w1_high_raw")[c]) for c, w in enumerate(widths)]
+        res_bf = [keep.tile([P, w, PACK], BF16, name=f"res_bf_{c}", align_bytes=64) for c, w in enumerate(widths)]
+        res_codes = [keep.tile([P, w], I32, name=f"res_codes_{c}", align_bytes=64) for c, w in enumerate(widths)]
 
         def make_hid(c):
-            nc.vector.tensor_tensor(grouped_by_lines(hid[c][:]), by_lines(hop[c]), by_lines(ob[c][:]), MULT)
+            nc.vector.tensor_tensor(grouped_by_pairs(hid[c][:]), by_pairs(hop[:, :, CHUNKS[c]]), by_pairs(ob[CHUNKS[c].start // HALF][:, :, CHUNKS[c].start % HALF : (CHUNKS[c].stop - 1) % HALF + 1]), MULT)
 
         def last_product(c):
             nc.vector.quantize_mx(hid_codes[c][:].bitcast(FP8X4), hid_scales[c][:], hid[c][:].rearrange("p c t -> p (c t)"))
-            for half in range(2):
-                bank = psum.tile([P, 2, CHUNK], F32, name="last_bank")
-                for k in range(2):
-                    cols = slice(P * (2 * half + k), P * (2 * half + k + 1))
+            per_bank = S // widths[c]
+            for first in range(0, PACK, per_bank):
+                bank = psum.tile([P, per_bank, widths[c]], F32, name="bank")
+                for k in range(per_bank):
+                    cols = slice(P * (first + k), P * (first + k + 1))
                     nc.tensor.matmul_mx(
                         bank[:, k, :], lhsT=w4q[0][:, cols].bitcast(FP8X4), lhsT_scale=w4q[1][:, cols],
                         rhs=hid_codes[c][:].bitcast(FP8X4), rhs_scale=hid_scales[c][:], start=True, stop=True,
                     )
-                nc.scalar.copy(res[c][:, 2 * half : 2 * half + 2, :], bank[:])
-            nc.sync.dma_start(out_rows[:, :, facts[c]], res[c][:])
+                nc.scalar.copy(res[c][:, first : first + per_bank, :], bank[:])
+                nc.sync.dma_start(out_rows[:, first : first + per_bank, CHUNKS[c]], res[c][:, first : first + per_bank, :])
 
         def round_res(c):
-            nc.vector.tensor_copy(grouped_by_lines(res_bf[c][:]), by_lines(res[c][:]))
+            nc.vector.tensor_copy(grouped_by_pairs(res_bf[c][:]), by_pairs(res[c][:]))
 
         def quantize_res(c):
-            nc.vector.quantize_mx(res_codes[c][:].bitcast(FP8X4), out_scales[:, facts[c]], res_bf[c][:].rearrange("p c t -> p (c t)"))
-            nc.sync.dma_start(out_words[:, facts[c]], res_codes[c][:])
+            nc.vector.quantize_mx(res_codes[c][:].bitcast(FP8X4), out_scales[:, CHUNKS[c]], res_bf[c][:].rearrange("p c t -> p (c t)"))
+            nc.sync.dma_start(out_words[:, CHUNKS[c]], res_codes[c][:])
 
         make_hid(0)
-        for c in chunks:
-            if c + 1 < len(chunks):
-                make_hid(c + 1)
-            last_product(c)
+        last_product(0)
+        make_hid(1)
+        make_hid(2)
+        last_product(1)
+        last_product(2)
         round_res(0)
-        for c in chunks:
-            if c + 1 < len(chunks):
-                round_res(c + 1)
-            quantize_res(c)
+        round_res(1)
+        quantize_res(0)
+        round_res(2)
+        quantize_res(1)
+        quantize_res(2)
         for q in range(4):
-            nc.sync.dma_start(out_2[0, 4 * q : 4 * q + 4, :].bitcast(I32), out_scales[32 * q : 32 * q + 4, :].bitcast(I32))
+            (nc.sync, nc.scalar)[q % 2].dma_start(out_2[0, 4 * q : 4 * q + 4, :].bitcast(I32), out_scales[32 * q : 32 * q + 4, :].bitcast(I32))

@@ -20,7 +20,7 @@ P = 128
 PACK = 4
 CHUNKS = (slice(0, 512), slice(512, 768), slice(768, 1024))
 HALF = 512
-PAIR = 2
+PAIR = 4
 SPARE = 16
 
 
@@ -111,7 +111,7 @@ def tile_picked_ytriple_mul_po_kernel(
                     rhs=picked[0][:].bitcast(FP8X4), rhs_scale=picked[1][:], start=True, stop=True,
                 )
                 row = keep.tile([P, offsets_at_once + SPARE], F32, name=f"{name}_{t}")
-                nc.gpsimd.memset(row[:, S:], 0.0)
+                nc.vector.memset(row[:, S:], 0.0)
                 if row_scale is None:
                     nc.scalar.copy(row[:, :S], bank[:])
                 else:
@@ -150,7 +150,6 @@ def tile_picked_ytriple_mul_po_kernel(
         for t in range(1, PACK):
             times_predicate(t, products[t])
             larger(t - 1, products[t - 1])
-        w4q = quantize_weight("w4", w4_bf16)
         larger(PACK - 1, products[PACK - 1])
         for first in range(0, U, HALF):
             for t in range(PACK):
@@ -199,6 +198,7 @@ def tile_picked_ytriple_mul_po_kernel(
             nc.sync.dma_start(out_words[:, CHUNKS[c]], res_codes[c][:])
 
         make_hid(0)
+        w4q = quantize_weight("w4", w4_bf16)
         last_product(0)
         make_hid(1)
         make_hid(2)

@@ -78,15 +78,13 @@ def tile_picked_ytriple_mul_po_kernel(
         to_sb = load_list("to", to)
         w4_raw = load_weight("w4", w4)
 
-        def round_weight(name, pieces, tag):
-            grouped = keep.tile([P, PACK, P, PACK], BF16, name=name + "_bf16", tag=tag, align_bytes=64)
+        def rounded_tile(name, tag):
+            return keep.tile([P, PACK, P, PACK], BF16, name=name + "_bf16", tag=tag, align_bytes=64)
+
+        def round_columns(copy, grouped, raw, first):
+            src = raw.rearrange("p j (m t) -> p m j t", t=PACK)
             dst = grouped[:].rearrange("p t m j -> p m j t")
-            first = 0
-            for raw, copy in pieces:
-                src = raw[:].rearrange("p j (m t) -> p m j t", t=PACK)
-                copy(dst[:, first : first + src.shape[1]], src)
-                first = first + src.shape[1]
-            return grouped
+            copy(dst[:, first // PACK : first // PACK + src.shape[1]], src)
 
         def quantize_weight(name, grouped):
             codes = keep.tile([P, 512], U32, name=name + "_codes", align_bytes=64)
@@ -101,7 +99,7 @@ def tile_picked_ytriple_mul_po_kernel(
             nc.vector.tensor_copy(words[:], table[:].bitcast(U32).indirect(lst[:]))
             return words, scales
 
-        def product(name, wq, picked, row_scale, offsets_at_once):
+        def product(name, wq, picked, row_scale, offsets_at_once, clear):
             rows = []
             for t in range(PACK):
                 cols = slice(P * t, P * (t + 1))
@@ -111,7 +109,7 @@ def tile_picked_ytriple_mul_po_kernel(
                     rhs=picked[0][:].bitcast(FP8X4), rhs_scale=picked[1][:], start=True, stop=True,
                 )
                 row = keep.tile([P, offsets_at_once + SPARE], F32, name=f"{name}_{t}")
-                nc.vector.memset(row[:, S:], 0.0)
+                clear(row[:, S:].bitcast(I32), 0)
                 if row_scale is None:
                     nc.scalar.copy(row[:, :S], bank[:])
                 else:
@@ -119,12 +117,19 @@ def tile_picked_ytriple_mul_po_kernel(
                 rows.append(row)
             return rows
 
-        w1q = quantize_weight("w1", round_weight("w1", [(w1_low, nc.scalar.copy), (w1_high, nc.vector.tensor_copy)], "w1_bf16"))
-        y = product("y", w1q, pick("x", x_table, x_plane, offs_sb), None, U)
+        w1_bf16 = rounded_tile("w1", "w1_bf16")
+        round_columns(nc.scalar.copy, w1_bf16, w1_low[:], 0)
+        round_columns(nc.vector.tensor_copy, w1_bf16, w1_high[:], 256)
+        w1q = quantize_weight("w1", w1_bf16)
+        y = product("y", w1q, pick("x", x_table, x_plane, offs_sb), None, U, nc.vector.memset)
         e_picked = pick("e", e_table, e_plane, prd_sb)
-        w2q = quantize_weight("w2", round_weight("w2", [(w2_raw, nc.vector.tensor_copy)], "w2_bf16"))
-        ye = product("ye", w2q, e_picked, None, U)
-        w3q = quantize_weight("w3", round_weight("w3", [(w3_raw, nc.vector.tensor_copy)], "w3_bf16"))
+        w2_bf16 = rounded_tile("w2", "w2_bf16")
+        round_columns(nc.vector.tensor_copy, w2_bf16, w2_raw[:], 0)
+        w2q = quantize_weight("w2", w2_bf16)
+        ye = product("ye", w2q, e_picked, None, U, nc.gpsimd.memset)
+        w3_bf16 = rounded_tile("w3", "w3_bf16")
+        round_columns(nc.vector.tensor_copy, w3_bf16, w3_raw[:], 0)
+        w3q = quantize_weight("w3", w3_bf16)
 
         sb_first = keep.tile([P, U], F32, name="sb_first")
         sb_rest = keep.tile([P, PACK - 1, U], F32, name="sb_rest", tag="e_picked", align_bytes=64)
@@ -143,14 +148,16 @@ def tile_picked_ytriple_mul_po_kernel(
 
         times_predicate(0, early[:])
         d_picked = pick("d", d_table, d_plane, obj_sb)
-        w4_bf16 = round_weight("w4", [(w4_raw, nc.scalar.copy)], "d_plane")
-        yd = product("yd", w3q, d_picked, unit_sb, HALF)
+        w4_bf16 = rounded_tile("w4", "d_plane")
+        round_columns(nc.scalar.copy, w4_bf16, w4_raw[:, :, :256], 0)
+        yd = product("yd", w3q, d_picked, unit_sb, HALF, nc.gpsimd.memset)
         late = keep.tile([P, PACK - 1, U], F32, name="late", tag="d_table", align_bytes=64)
         products = [early[:]] + [late[:, t, :] for t in range(PACK - 1)]
         for t in range(1, PACK):
             times_predicate(t, products[t])
             larger(t - 1, products[t - 1])
         larger(PACK - 1, products[PACK - 1])
+        round_columns(nc.vector.tensor_copy, w4_bf16, w4_raw[:, :, 256:], 256)
         for first in range(0, U, HALF):
             for t in range(PACK):
                 nc.scalar.activation(ob[first // HALF][:, t, :], yd[t][:].indirect(to_sb[:, first // 16 : (first + HALF) // 16]), COPY)

from contextlib import ExitStack

import concourse.mybir as mybir

K, S, U = 512, 512, 1024
FLOPS = 2 * K * 512 * (3 * S + U)

F32 = mybir.dt.float32
BF16 = mybir.dt.bfloat16
I32 = mybir.dt.int32
U32 = mybir.dt.uint32
U16 = mybir.dt.uint16
U8 = mybir.dt.uint8
FP8X4 = mybir.dt.float8_e4m3fn_x4
COPY = mybir.ActivationFunctionType.Copy
MULT = mybir.AluOpType.mult
MAX = mybir.AluOpType.max

P = 128
PACK = 4
CHUNKS = (slice(0, 512), slice(512, 768), slice(768, 1024))
HALF = 512
PAIR = 4
SPARE = 16


def tile_picked_ytriple_mul_po_kernel(
    tc, x_words, x_scales, w1, e_words, e_scales, w2, d_words, d_scales, w3, unit, w4,
    offs, prd, obj, ts, tp, to, out_0, out_1, out_2,
):
    nc = tc.nc
    with ExitStack() as ctx:
        keep = ctx.enter_context(tc.tile_pool(name="keep", bufs=1))
        psum = ctx.enter_context(tc.psum_pool(name="psum", bufs=8))

        def load_list(name, src):
            t = keep.tile(list(src.shape), U16, name=name)
            nc.sync.dma_start(t[:], src)
            return t

        def load_weight(name, w):
            raw = keep.tile([P, PACK, w.shape[1]], F32, name=name + "_raw", tag=name + "_raw")
            nc.sync.dma_start(raw[:], w.rearrange("(p j) c -> p j c", j=PACK))
            return raw

        def load_scales(name, scales, queue):
            width = scales.shape[2]
            plane = keep.tile([P, width], U8, name=name + "_plane", tag=name + "_plane", align_bytes=64)
            nc.vector.memset(plane[:, : width // 2].bitcast(I32), 0)
            nc.gpsimd.memset(plane[:, width // 2 :].bitcast(I32), 0)
            for q in range(4):
                queue.dma_start(plane[32 * q : 32 * q + 4, :].bitcast(I32), scales[0, 4 * q : 4 * q + 4, :].bitcast(I32))
            return plane

        def load_words(name, words):
            width = words.shape[2]
            table = keep.tile([P, width], I32, name=name + "_table", tag=name + "_table", align_bytes=64)
            nc.sync.dma_start(table[:], words[0].rearrange("p n t -> p (n t)").bitcast(I32))
            return table

        w1_low = load_weight("w1_low", w1[:, :256])
        w1_high = load_weight("w1_high", w1[:, 256:])
        offs_sb = load_list("offs", offs)
        x_plane = load_scales("x", x_scales, nc.sync)
        x_table = load_words("x", x_words)
        e_table = load_words("e", e_words)
        prd_sb = load_list("prd", prd)
        e_plane = load_scales("e", e_scales, nc.sync)
        w2_raw = load_weight("w2", w2)
        ts_sb = load_list("ts", ts)
        tp_sb = load_list("tp", tp)
        w3_raw = load_weight("w3", w3)
        obj_sb = load_list("obj", obj)
        d_plane = load_scales("d", d_scales, nc.sync)
        d_table = load_words("d", d_words)
        unit_sb = keep.tile([P, PACK], F32, name="unit_sb")
        nc.sync.dma_start(unit_sb[:], unit.rearrange("(p t) o -> p (t o)", t=PACK))
        to_sb = load_list("to", to)
        w4_raw = load_weight("w4", w4)

        def rounded_tile(name, tag):
            return keep.tile([P, PACK, P, PACK], BF16, name=name + "_bf16", tag=tag, align_bytes=64)

        def round_columns(copy, grouped, raw, first):
            src = raw.rearrange("p j (m t) -> p m j t", t=PACK)
            dst = grouped[:].rearrange("p t m j -> p m j t")
            copy(dst[:, first // PACK : first // PACK + src.shape[1]], src)

        def quantize_weight(name, grouped):
            codes = keep.tile([P, 512], U32, name=name + "_codes", align_bytes=64)
            scales = keep.tile([P, 512], U8, name=name + "_scales", align_bytes=64)
            nc.vector.quantize_mx(codes[:].bitcast(FP8X4), scales[:], grouped[:].rearrange("p t m j -> p (t m j)"))
            return codes, scales

        def pick(name, table, plane, lst):
            scales = keep.tile([P, S], U8, name=name + "_picked_scales", align_bytes=64)
            nc.vector.tensor_copy(scales[:], plane[:].indirect(lst[:]))
            words = keep.tile([P, S], U32, name=name + "_picked_words", tag=name + "_picked", align_bytes=64)
            nc.vector.tensor_copy(words[:], table[:].bitcast(U32).indirect(lst[:]))
            return words, scales

        def product(name, wq, picked, row_scale, offsets_at_once, clear):
            rows = []
            for t in range(PACK):
                cols = slice(P * t, P * (t + 1))
                bank = psum.tile([P, S], F32, name="bank")
                nc.tensor.matmul_mx(
                    bank[:], lhsT=wq[0][:, cols].bitcast(FP8X4), lhsT_scale=wq[1][:, cols],
                    rhs=picked[0][:].bitcast(FP8X4), rhs_scale=picked[1][:], start=True, stop=True,
                )
                row = keep.tile([P, offsets_at_once + SPARE], F32, name=f"{name}_{t}")
                clear(row[:, S:].bitcast(I32), 0)
                if row_scale is None:
                    nc.scalar.copy(row[:, :S], bank[:])
                else:
                    nc.scalar.activation(row[:, :S], bank[:], COPY, scale=row_scale[:, t : t + 1])
                rows.append(row)
            return rows

        w1_bf16 = rounded_tile("w1", "w1_bf16")
        round_columns(nc.scalar.copy, w1_bf16, w1_low[:], 0)
        round_columns(nc.vector.tensor_copy, w1_bf16, w1_high[:], 256)
        w1q = quantize_weight("w1", w1_bf16)
        y = product("y", w1q, pick("x", x_table, x_plane, offs_sb), None, U, nc.vector.memset)
        e_picked = pick("e", e_table, e_plane, prd_sb)
        w2_bf16 = rounded_tile("w2", "w2_bf16")
        round_columns(nc.vector.tensor_copy, w2_bf16, w2_raw[:], 0)
        w2q = quantize_weight("w2", w2_bf16)
        ye = product("ye", w2q, e_picked, None, U, nc.gpsimd.memset)
        w3_bf16 = rounded_tile("w3", "w3_bf16")
        round_columns(nc.vector.tensor_copy, w3_bf16, w3_raw[:], 0)
        w3q = quantize_weight("w3", w3_bf16)

        sb_first = keep.tile([P, U], F32, name="sb_first")
        sb_rest = keep.tile([P, PACK - 1, U], F32, name="sb_rest", tag="e_picked", align_bytes=64)
        sb = [sb_first[:]] + [sb_rest[:, t, :] for t in range(PACK - 1)]
        early = keep.tile([P, U], F32, name="early", tag="w3_bf16", align_bytes=64)
        hop = keep.tile([P, PACK, U], F32, name="hop")
        ob = [keep.tile([P, PACK, HALF], F32, name=f"ob_{h}") for h in range(U // HALF)]
        for t in range(PACK):
            nc.scalar.activation(sb[t], y[t][:].indirect(ts_sb[:]), COPY)

        def times_predicate(t, dst):
            nc.vector.tensor_tensor(dst, ye[t][:].indirect(tp_sb[:]), sb[t], MULT)

        def larger(t, prod):
            nc.vector.scalar_tensor_tensor(hop[:, t, :], sb[t], 0.4, prod, MULT, MAX)

        times_predicate(0, early[:])
        d_picked = pick("d", d_table, d_plane, obj_sb)
        w4_bf16 = rounded_tile("w4", "d_plane")
        round_columns(nc.scalar.copy, w4_bf16, w4_raw[:, :, :256], 0)
        yd = product("yd", w3q, d_picked, unit_sb, HALF, nc.gpsimd.memset)
        late = keep.tile([P, PACK - 1, U], F32, name="late", tag="d_table", align_bytes=64)
        products = [early[:]] + [late[:, t, :] for t in range(PACK - 1)]
        for t in range(1, PACK):
            times_predicate(t, products[t])
            larger(t - 1, products[t - 1])
        larger(PACK - 1, products[PACK - 1])
        round_columns(nc.vector.tensor_copy, w4_bf16, w4_raw[:, :, 256:], 256)
        for first in range(0, U, HALF):
            for t in range(PACK):
                nc.scalar.activation(ob[first // HALF][:, t, :], yd[t][:].indirect(to_sb[:, first // 16 : (first + HALF) // 16]), COPY)

        out_scales = keep.tile([P, U], U8, name="out_scales", align_bytes=64)
        out_rows = out_0.rearrange("(p t) r -> p t r", t=PACK)
        out_words = out_1[0].rearrange("p n t -> p (n t)").bitcast(I32)

        def by_pairs(planes):
            return planes.rearrange("p t (c i) -> p c t i", i=PAIR)

        def grouped_by_pairs(grouped):
            return grouped.rearrange("p (c i) t -> p c t i", i=PAIR)

        widths = [facts.stop - facts.start for facts in CHUNKS]
        hid = [keep.tile([P, w, PACK], BF16, name=f"hid_{c}", align_bytes=64) for c, w in enumerate(widths)]
        hid_codes = [keep.tile([P, w], U32, name=f"hid_codes_{c}", align_bytes=64) for c, w in enumerate(widths)]
        hid_scales = [keep.tile([P, w], U8, name=f"hid_scales_{c}", align_bytes=64) for c, w in enumerate(widths)]
        res = [keep.tile([P, PACK, w], F32, name=f"res_{c}", tag=("w2_raw", "w1_low_raw", "w1_high_raw")[c]) for c, w in enumerate(widths)]
        res_bf = [keep.tile([P, w, PACK], BF16, name=f"res_bf_{c}", align_bytes=64) for c, w in enumerate(widths)]
        res_codes = [keep.tile([P, w], I32, name=f"res_codes_{c}", align_bytes=64) for c, w in enumerate(widths)]

        def make_hid(c):
            nc.vector.tensor_tensor(grouped_by_pairs(hid[c][:]), by_pairs(hop[:, :, CHUNKS[c]]), by_pairs(ob[CHUNKS[c].start // HALF][:, :, CHUNKS[c].start % HALF : (CHUNKS[c].stop - 1) % HALF + 1]), MULT)

        def last_product(c):
            nc.vector.quantize_mx(hid_codes[c][:].bitcast(FP8X4), hid_scales[c][:], hid[c][:].rearrange("p c t -> p (c t)"))
            per_bank = S // widths[c]
            for first in range(0, PACK, per_bank):
                bank = psum.tile([P, per_bank, widths[c]], F32, name="bank")
                for k in range(per_bank):
                    cols = slice(P * (first + k), P * (first + k + 1))
                    nc.tensor.matmul_mx(
                        bank[:, k, :], lhsT=w4q[0][:, cols].bitcast(FP8X4), lhsT_scale=w4q[1][:, cols],
                        rhs=hid_codes[c][:].bitcast(FP8X4), rhs_scale=hid_scales[c][:], start=True, stop=True,
                    )
                nc.scalar.copy(res[c][:, first : first + per_bank, :], bank[:])
                nc.sync.dma_start(out_rows[:, first : first + per_bank, CHUNKS[c]], res[c][:, first : first + per_bank, :])

        def round_res(c):
            nc.vector.tensor_copy(grouped_by_pairs(res_bf[c][:]), by_pairs(res[c][:]))

        def quantize_res(c):
            nc.vector.quantize_mx(res_codes[c][:].bitcast(FP8X4), out_scales[:, CHUNKS[c]], res_bf[c][:].rearrange("p c t -> p (c t)"))
            nc.sync.dma_start(out_words[:, CHUNKS[c]], res_codes[c][:])

        make_hid(0)
        w4q = quantize_weight("w4", w4_bf16)
        last_product(0)
        make_hid(1)
        make_hid(2)
        last_product(1)
        last_product(2)
        round_res(0)
        round_res(1)
        quantize_res(0)
        round_res(2)
        quantize_res(1)
        quantize_res(2)
        for q in range(4):
            (nc.sync, nc.scalar)[q % 2].dma_start(out_2[0, 4 * q : 4 * q + 4, :].bitcast(I32), out_scales[32 * q : 32 * q + 4, :].bitcast(I32))
